import numpy as np
import ml_dtypes


def mxq(x, axis, fmt="e4m3"):
    dtype, down = {"e4m3": (ml_dtypes.float8_e4m3fn, 7), "e5m2": (ml_dtypes.float8_e5m2, 14)}[fmt]
    v = np.moveaxis(np.asarray(x, np.float32).astype(ml_dtypes.bfloat16).astype(np.float64), axis, -1)
    blocks = v.reshape(v.shape[:-1] + (-1, 32))
    amax = np.abs(blocks).max(-1, keepdims=True)
    byte = np.maximum(np.where(amax > 0, np.frexp(amax)[1] - 1 + 127, 0) - down, 1)
    scale = np.exp2(byte - 127.0)
    codes = (blocks / scale).astype(np.float32).astype(dtype).astype(np.float64)
    return np.moveaxis((codes * scale).reshape(v.shape), -1, axis)


WIDE = False


def mx_kscale(k):
    if not WIDE:
        return np.ones(k)
    levels = np.array([10, -10, 5, -5, 0])
    if k % 512:
        return np.exp2(np.random.permutation(np.resize(levels, k // 32))).repeat(32)
    a = np.empty((k // 512, 16))
    for p in range(k // 512):
        a[p, :8] = np.random.permutation(np.resize(levels, 8))
        for g in range(8):
            far = levels[np.abs(levels - a[p, g]) >= 10]
            a[p, g + 8] = far[np.random.randint(len(far))]
    return np.exp2(a.ravel()).repeat(32)


def f64(x):
    return np.asarray(x).astype(np.float64)


def striped(idx):
    return np.tile(idx.reshape(-1, 16).T, (8, 1)).astype(np.uint16)


def unstriped(offs):
    return offs[:16].T.reshape(-1).astype(np.int64)


def striped8(idx):
    return np.concatenate([x.reshape(-1, 16).T for x in idx]).astype(np.uint16)


def runs(offs, k):
    lists = np.stack([offs[16 * r : 16 * r + 16].T.reshape(-1) for r in range(8)]).astype(np.int64)
    return lists[np.arange(k) % 512 // 64]


def pack_weight(w):
    k, n = w.shape
    w = f64(np.asarray(w, np.float32).astype(ml_dtypes.bfloat16)).reshape(k // 32, 32, n)
    amax = np.abs(w).max(1)
    byte = np.clip(np.where(amax > 0, np.frexp(amax)[1] - 1 + 127 - 7, 1), 1, 254)
    scaled = (w * np.exp2(127.0 - byte)[:, None, :]).reshape(k, n).astype(np.float32)
    words = np.ascontiguousarray(scaled.reshape(k // 512, 128, 4, n).transpose(0, 1, 3, 2)).astype(ml_dtypes.float8_e4m3fn).view(np.uint8)
    return words, np.ascontiguousarray(byte.astype(np.uint8).reshape(k // 512, 16, n))


def unpack_weight(words, scales):
    g, p, n, _ = words.shape
    vals = np.ascontiguousarray(words).view(ml_dtypes.float8_e4m3fn).astype(np.float64) * np.repeat(np.exp2(scales.astype(np.float64) - 127.0), 8, axis=1)[..., None]
    return vals.transpose(0, 1, 3, 2).reshape(g * 512, n)


K, T, S, H, J, W = 512, 2048, 512, 512, 512, 256


def setup_inputs():
    n = np.random.standard_normal
    s = mx_kscale(K)[:, None]
    u = mx_kscale(S)
    packed_xT = pack_weight(n((K, T)) * s)
    perm = np.stack([np.random.permutation(S) for _ in range(8)])
    return {
        "x_words": packed_xT[0],
        "x_scales": packed_xT[1],
        "w1": (n((K, H)) / np.sqrt(K) / s).astype(np.float32),
        "tab": n((H, J)).astype(np.float32),
        "ga": (np.random.uniform(0.5, 1.5, (H, 1)) * u[:, None]).astype(np.float32),
        "gb": (np.random.uniform(0.5, 1.5, (H, 1)) / u[:, None]).astype(np.float32),
        "offs": striped(np.random.permutation(T)[:S]),
        "n1": striped8(np.stack([np.random.permutation(S) for _ in range(8)])),
        "n2": striped8(np.stack([np.random.permutation(S) for _ in range(8)])),
        "n3": striped8(np.stack([np.random.permutation(S) for _ in range(8)])),
        "n4": striped8(np.random.randint(0, J, (8, S))),
        "n5": striped8(np.stack([np.random.permutation(S) for _ in range(8)])),
        "n6": striped8(perm[:, :W]),
        "n7": striped8(perm[:, W:]),
    }


def reference(x_words, x_scales, w1, tab, ga, gb, offs, n1, n2, n3, n4, n5, n6, n7):
    xq = unpack_weight(x_words, x_scales)[:, unstriped(offs)]
    y = mxq(f64(w1), 0, "e4m3").T @ xq
    st = y - (y[np.arange(H)[:, None], runs(n1, H)])
    su = np.maximum(st, st[np.arange(H)[:, None], runs(n2, H)])
    z = f64(ga) * (su + 0.5 * (su[np.arange(H)[:, None], runs(n3, H)]))
    z2 = f64(gb) * (np.maximum(y + f64(tab)[np.arange(H)[:, None], runs(n4, H)], y[np.arange(H)[:, None], runs(n5, H)]))
    s = 0.0625 * ((mxq(z, 0, "e4m3").T @ mxq(z2, 0, "e4m3")))
    pb = s[np.arange(S)[:, None], runs(n7, S)]
    pa = s[np.arange(S)[:, None], runs(n6, S)]
    rb = pb - (0.5 * pa)
    ra = np.sqrt((pa) ** 2 + (pb) ** 2 + 0.25)
    ds = np.zeros((S, S))
    ds[np.arange(S)[:, None], runs(n6, S)] = ra
    out = ds.copy()
    out[np.arange(S)[:, None], runs(n7, S)] = rb
    return out

@@ -1,0 +1,183 @@
+from contextlib import ExitStack
+
+import concourse.mybir as mybir
+
+K, T, S, H, W = 512, 2048, 512, 512, 256
+FLOPS = 2 * K * H * S + 2 * H * S * S
+
+F32 = mybir.dt.float32
+BF16 = mybir.dt.bfloat16
+I32 = mybir.dt.int32
+U32 = mybir.dt.uint32
+U16 = mybir.dt.uint16
+U8 = mybir.dt.uint8
+FP8X4 = mybir.dt.float8_e4m3fn_x4
+ALU = mybir.AluOpType
+ACT = mybir.ActivationFunctionType
+
+P = 128
+PACK = 4
+WIDE = 2 * S
+
+
+def tile_picked_selfthreekindpolar_none_p_kernel(
+    tc, x_words, x_scales, w1, tab, ga, gb, offs, n1, n2, n3, n4, n5, n6, n7, out
+):
+    nc = tc.nc
+    with ExitStack() as ctx:
+        lists = ctx.enter_context(tc.tile_pool(name="lists", bufs=1))
+        sb = ctx.enter_context(tc.tile_pool(name="sb", bufs=1))
+        psum = ctx.enter_context(tc.psum_pool(name="psum", bufs=1))
+
+        def load_list(src, name):
+            t = lists.tile(list(src.shape), U16, name=name)
+            nc.sync.dma_start(t[:], src)
+            return t
+
+        def planes(name, width, dtype=F32):
+            return [sb.tile([P, width], dtype, name=f"{name}{t}", align_bytes=64) for t in range(PACK)]
+
+        quarter = sb.tile([P, 1], F32, name="quarter")
+        warm = sb.tile([P, 1], F32, name="warm")
+        nc.gpsimd.memset(quarter[:], 0.25)
+        nc.scalar.activation(warm[:], quarter[:], ACT.Sqrt)
+
+        xs = sb.tile([P, T], U8, name="xs", align_bytes=64)
+        nc.vector.memset(xs[:].bitcast(I32), 0)
+        xw = sb.tile([P, T], U32, name="xw", align_bytes=64)
+        nc.sync.dma_start(xw[:].bitcast(I32), x_words[0].rearrange("p n t -> p (n t)").bitcast(I32))
+        l_offs = load_list(offs, "l_offs")
+        for q in range(4):
+            nc.sync.dma_start(xs[32 * q : 32 * q + 4, :].bitcast(I32), x_scales[0, 4 * q : 4 * q + 4, :].bitcast(I32))
+        w_rows = w1.rearrange("(p j) c -> p j c", j=PACK)
+        w_raw = [sb.tile([P, PACK, H // 2], F32, name=f"w_raw{h}") for h in range(2)]
+        for h in range(2):
+            nc.sync.dma_start(w_raw[h][:], w_rows[:, :, h * 256 : (h + 1) * 256])
+        l1 = load_list(n1, "l1")
+        l5 = load_list(n5, "l5")
+        tab_rows = tab.rearrange("(p t) c -> p t c", t=PACK)
+        tab_w = planes("tab_w", WIDE)
+        nc.sync.dma_start(tab_w[0][:, :S], tab_rows[:, 0, :])
+        l2 = load_list(n2, "l2")
+        l4 = load_list(n4, "l4")
+        for t in range(1, PACK):
+            nc.sync.dma_start(tab_w[t][:, :S], tab_rows[:, t, :])
+        ga_sb = sb.tile([P, PACK], F32, name="ga_sb")
+        gb_sb = sb.tile([P, PACK], F32, name="gb_sb")
+        nc.sync.dma_start(ga_sb[:], ga.rearrange("(p t) o -> p (t o)", t=PACK))
+        nc.sync.dma_start(gb_sb[:], gb.rearrange("(p t) o -> p (t o)", t=PACK))
+        l3 = load_list(n3, "l3")
+        l6 = load_list(n6, "l6")
+        l7 = load_list(n7, "l7")
+
+        sq_w = planes("sq_w", S)
+        for t in range(PACK):
+            nc.gpsimd.memset(sq_w[t][:], 0.0)
+        ga_neg = sb.tile([P, PACK], F32, name="ga_neg")
+        ga_neg_half = sb.tile([P, PACK], F32, name="ga_neg_half")
+        nc.scalar.mul(ga_neg[:], ga_sb[:], -1.0)
+        nc.scalar.mul(ga_neg_half[:], ga_sb[:], -0.5)
+
+        xw_p = sb.tile([P, S], U32, name="xw_p", align_bytes=64)
+        xs_p = sb.tile([P, S], U8, name="xs_p", align_bytes=64)
+        nc.vector.tensor_copy(xs_p[:], xs[:].indirect(l_offs[:]))
+        nc.vector.tensor_copy(xw_p[:], xw[:].indirect(l_offs[:]))
+
+        w_bf = sb.tile([P, PACK * H], BF16, name="w_bf", align_bytes=64)
+        w_dst = w_bf[:].rearrange("p (t m j) -> p m j t", t=PACK, j=PACK)
+        nc.scalar.copy(w_dst[:, 0:64], w_raw[0][:].rearrange("p j (m t) -> p m j t", t=PACK))
+        nc.vector.tensor_copy(w_dst[:, 64:128], w_raw[1][:].rearrange("p j (m t) -> p m j t", t=PACK))
+        w_c = sb.tile([P, H], U32, name="w_c", align_bytes=64)
+        w_s = sb.tile([P, H], U8, name="w_s", align_bytes=64)
+        y_ps = [psum.tile([P, S], F32, name=f"y_ps{t}") for t in range(PACK)]
+        y_w = planes("y_w", WIDE)
+        y_c = planes("y_c", S)
+        for g in range(2):
+            cols = slice(g * 256, (g + 1) * 256)
+            nc.vector.quantize_mx(out=w_c[:, cols].bitcast(FP8X4), scales=w_s[:, cols], in_=w_bf[:, g * 1024 : (g + 1) * 1024])
+        for t in range(PACK):
+            cols = slice(t * P, (t + 1) * P)
+            nc.tensor.matmul_mx(out=y_ps[t][:], lhsT=w_c[:, cols].bitcast(FP8X4), lhsT_scale=w_s[:, cols],
+                                rhs=xw_p[:].bitcast(FP8X4), rhs_scale=xs_p[:], start=True, stop=True)
+            nc.scalar.copy(y_w[t][:, :S], y_ps[t][:])
+            nc.scalar.copy(y_c[t][:], y_ps[t][:])
+
+        nst_w = planes("nst_w", WIDE)
+        y5 = planes("y5", S)
+        nst2 = planes("nst2", S)
+        ytab = planes("ytab", S)
+        nsu = planes("nsu", S)
+        big = planes("big", S)
+        zs = planes("zs", S)
+        zh_w = planes("zh_w", WIDE)
+        z2_f = sb.tile([P, PACK, S], F32, name="z2_f")
+        z_f = sb.tile([P, PACK, S], F32, name="z_f")
+        for t in range(PACK):
+            nc.vector.tensor_tensor(nst_w[t][:, :S], y_w[t][:].indirect(l1[:]), y_c[t][:], ALU.subtract)
+            nc.vector.tensor_copy(y5[t][:], y_w[t][:].indirect(l5[:]))
+        for t in range(PACK):
+            nc.vector.tensor_tensor(ytab[t][:], tab_w[t][:].indirect(l4[:]), y_c[t][:], ALU.add)
+            nc.vector.tensor_copy(nst2[t][:], nst_w[t][:].indirect(l2[:]))
+        for t in range(PACK):
+            nc.vector.tensor_tensor(big[t][:], ytab[t][:], y5[t][:], ALU.max)
+            nc.scalar.activation(z2_f[:, t, :], big[t][:], ACT.Copy, scale=gb_sb[:, t : t + 1])
+        for t in range(PACK):
+            nc.vector.tensor_tensor(nsu[t][:], nst_w[t][:, :S], nst2[t][:], ALU.min)
+            nc.scalar.activation(zh_w[t][:, :S], nsu[t][:], ACT.Copy, scale=ga_neg_half[:, t : t + 1])
+            nc.scalar.activation(zs[t][:], nsu[t][:], ACT.Copy, scale=ga_neg[:, t : t + 1])
+
+        z2_bf = sb.tile([P, PACK * S], BF16, name="z2_bf", align_bytes=64)
+        nc.scalar.copy(z2_bf[:].rearrange("p (c i t) -> p c t i", i=4, t=PACK),
+                       z2_f[:].rearrange("p t (c i) -> p c t i", i=4))
+        z2_c = sb.tile([P, S], U32, name="z2_c", align_bytes=64)
+        z2_s = sb.tile([P, S], U8, name="z2_s", align_bytes=64)
+
+        z_bf = sb.tile([P, PACK * S], BF16, name="z_bf", align_bytes=64)
+        z_dst = z_bf[:].rearrange("p (u m t) -> p m t u", u=PACK, t=PACK)
+        z_src = z_f[:].rearrange("p t (m u) -> p m t u", u=PACK)
+        for h in range(2):
+            cols = slice(h * 256, (h + 1) * 256)
+            for t in range(PACK):
+                nc.vector.tensor_tensor(z_f[:, t, cols], zh_w[t][:].indirect(l3[:, h * 16 : (h + 1) * 16]), zs[t][:, cols], ALU.add)
+            if h == 0:
+                nc.scalar.copy(z_dst[:, 0:64], z_src[:, 0:64])
+                nc.vector.quantize_mx(out=z2_c[:].bitcast(FP8X4), scales=z2_s[:], in_=z2_bf[:])
+            else:
+                nc.vector.tensor_copy(z_dst[:, 64:128], z_src[:, 64:128])
+
+        z_c = planes("z_c", P, U32)
+        z_s = planes("z_s", P, U8)
+        s_ps = [psum.tile([P, S], F32, name=f"s_ps{u}") for u in range(PACK)]
+        s_w = planes("s_w", S)
+        pab = planes("pab", S)
+        sq = planes("sq", S)
+        half = planes("half", W)
+        res = planes("res", S)
+        out_rows = out.rearrange("(p u) c -> p u c", u=PACK)
+        for u in range(PACK):
+            nc.vector.quantize_mx(out=z_c[u][:].bitcast(FP8X4), scales=z_s[u][:], in_=z_bf[:, u * S : (u + 1) * S])
+            nc.tensor.matmul_mx(out=s_ps[u][:], lhsT=z_c[u][:].bitcast(FP8X4), lhsT_scale=z_s[u][:],
+                                rhs=z2_c[:].bitcast(FP8X4), rhs_scale=z2_s[:], start=True, stop=True)
+            nc.scalar.mul(s_w[u][:], s_ps[u][:], 0.0625)
+
+        def fetch(u):
+            nc.vector.tensor_copy(pab[u][:, :W], s_w[u][:].indirect(l6[:]))
+            nc.vector.tensor_copy(pab[u][:, W:], s_w[u][:].indirect(l7[:]))
+            nc.scalar.activation(sq[u][:], pab[u][:], ACT.Square)
+            nc.scalar.mul(half[u][:], pab[u][:, :W], -0.5)
+
+        def put_radius(u):
+            nc.vector.tensor_tensor(sq_w[u][:].indirect(l6[:]), sq[u][:, :W], sq[u][:, W:], ALU.add)
+            nc.scalar.activation(res[u][:], sq_w[u][:], ACT.Sqrt, bias=quarter[:])
+
+        def put_rest(u):
+            nc.vector.tensor_tensor(res[u][:].indirect(l7[:]), pab[u][:, W:], half[u][:], ALU.add)
+            nc.sync.dma_start(out_rows[:, u, :], res[u][:])
+
+        for step in range(PACK + 2):
+            if step < PACK:
+                fetch(step)
+            if 1 <= step <= PACK:
+                put_radius(step - 1)
+            if step >= 2:
+                put_rest(step - 2)

@@ -1,6 +1,7 @@
 from contextlib import ExitStack
 
 import concourse.mybir as mybir
+from concourse.masks import make_identity
 
 K, T, S, H, W = 512, 2048, 512, 512, 256
 FLOPS = 2 * K * H * S + 2 * H * S * S
@@ -43,29 +44,32 @@ def tile_picked_selfthreekindpolar_none_p_kernel(
         nc.scalar.activation(warm[:], quarter[:], ACT.Sqrt)
 
         xs = sb.tile([P, T], U8, name="xs", align_bytes=64)
-        nc.vector.memset(xs[:].bitcast(I32), 0)
-        xw = sb.tile([P, T], U32, name="xw", align_bytes=64)
-        nc.sync.dma_start(xw[:].bitcast(I32), x_words[0].rearrange("p n t -> p (n t)").bitcast(I32))
-        l_offs = load_list(offs, "l_offs")
-        for q in range(4):
-            nc.sync.dma_start(xs[32 * q : 32 * q + 4, :].bitcast(I32), x_scales[0, 4 * q : 4 * q + 4, :].bitcast(I32))
-        w_rows = w1.rearrange("(p j) c -> p j c", j=PACK)
-        w_raw = [sb.tile([P, PACK, H // 2], F32, name=f"w_raw{h}") for h in range(2)]
-        for h in range(2):
-            nc.sync.dma_start(w_raw[h][:], w_rows[:, :, h * 256 : (h + 1) * 256])
-        l1 = load_list(n1, "l1")
-        l5 = load_list(n5, "l5")
+        nc.gpsimd.memset(xs[:].bitcast(I32), 0)
+        ident = sb.tile([P, P], F32, name="ident")
+        make_identity(nc, ident[:])
         tab_rows = tab.rearrange("(p t) c -> p t c", t=PACK)
         tab_w = planes("tab_w", WIDE)
         nc.sync.dma_start(tab_w[0][:, :S], tab_rows[:, 0, :])
-        l2 = load_list(n2, "l2")
         l4 = load_list(n4, "l4")
-        for t in range(1, PACK):
+        l_offs = load_list(offs, "l_offs")
+        l5 = load_list(n5, "l5")
+        l1 = load_list(n1, "l1")
+        for t in range(1, 3):
             nc.sync.dma_start(tab_w[t][:, :S], tab_rows[:, t, :])
+        w_rows = w1.rearrange("(p j) c -> p j c", j=PACK)
+        w_raw = [sb.tile([P, PACK, H // 2], F32, name=f"w_raw{h}") for h in range(2)]
+        nc.sync.dma_start(w_raw[0][:], w_rows[:, :, :256])
+        for q in range(4):
+            nc.sync.dma_start(xs[32 * q : 32 * q + 4, :].bitcast(I32), x_scales[0, 4 * q : 4 * q + 4, :].bitcast(I32))
+        nc.sync.dma_start(w_raw[1][:], w_rows[:, :, 256:])
+        xw = sb.tile([P, T], U32, name="xw", align_bytes=64)
+        nc.sync.dma_start(xw[:].bitcast(I32), x_words[0].rearrange("p n t -> p (n t)").bitcast(I32))
+        nc.sync.dma_start(tab_w[3][:, :S], tab_rows[:, 3, :])
+        l2 = load_list(n2, "l2")
         ga_sb = sb.tile([P, PACK], F32, name="ga_sb")
         gb_sb = sb.tile([P, PACK], F32, name="gb_sb")
-        nc.sync.dma_start(ga_sb[:], ga.rearrange("(p t) o -> p (t o)", t=PACK))
         nc.sync.dma_start(gb_sb[:], gb.rearrange("(p t) o -> p (t o)", t=PACK))
+        nc.sync.dma_start(ga_sb[:], ga.rearrange("(p t) o -> p (t o)", t=PACK))
         l3 = load_list(n3, "l3")
         l6 = load_list(n6, "l6")
         l7 = load_list(n7, "l7")
@@ -73,81 +77,123 @@ def tile_picked_selfthreekindpolar_none_p_kernel(
         sq_w = planes("sq_w", S)
         for t in range(PACK):
             nc.gpsimd.memset(sq_w[t][:], 0.0)
+        tg = planes("tg", S)
+        for t in range(3):
+            nc.vector.tensor_copy(tg[t][:], tab_w[t][:].indirect(l4[:]))
         ga_neg = sb.tile([P, PACK], F32, name="ga_neg")
         ga_neg_half = sb.tile([P, PACK], F32, name="ga_neg_half")
-        nc.scalar.mul(ga_neg[:], ga_sb[:], -1.0)
-        nc.scalar.mul(ga_neg_half[:], ga_sb[:], -0.5)
 
         xw_p = sb.tile([P, S], U32, name="xw_p", align_bytes=64)
         xs_p = sb.tile([P, S], U8, name="xs_p", align_bytes=64)
         nc.vector.tensor_copy(xs_p[:], xs[:].indirect(l_offs[:]))
-        nc.vector.tensor_copy(xw_p[:], xw[:].indirect(l_offs[:]))
 
         w_bf = sb.tile([P, PACK * H], BF16, name="w_bf", align_bytes=64)
         w_dst = w_bf[:].rearrange("p (t m j) -> p m j t", t=PACK, j=PACK)
         nc.scalar.copy(w_dst[:, 0:64], w_raw[0][:].rearrange("p j (m t) -> p m j t", t=PACK))
-        nc.vector.tensor_copy(w_dst[:, 64:128], w_raw[1][:].rearrange("p j (m t) -> p m j t", t=PACK))
+        w_late = w_raw[1][:].rearrange("p j (m t) -> p m j t", t=PACK)
+        nc.scalar.copy(w_dst[:, 64:96], w_late[:, 0:32])
+        nc.vector.tensor_copy(w_dst[:, 96:128], w_late[:, 32:64])
         w_c = sb.tile([P, H], U32, name="w_c", align_bytes=64)
         w_s = sb.tile([P, H], U8, name="w_s", align_bytes=64)
-        y_ps = [psum.tile([P, S], F32, name=f"y_ps{t}") for t in range(PACK)]
         y_w = planes("y_w", WIDE)
         y_c = planes("y_c", S)
-        for g in range(2):
-            cols = slice(g * 256, (g + 1) * 256)
-            nc.vector.quantize_mx(out=w_c[:, cols].bitcast(FP8X4), scales=w_s[:, cols], in_=w_bf[:, g * 1024 : (g + 1) * 1024])
-        for t in range(PACK):
+        nc.vector.quantize_mx(out=w_c[:].bitcast(FP8X4), scales=w_s[:], in_=w_bf[:])
+        for h in range(2):
+            nc.vector.tensor_copy(xw_p[:, h * W : (h + 1) * W], xw[:].indirect(l_offs[:, h * 16 : (h + 1) * 16]))
+        nc.vector.tensor_copy(tg[3][:], tab_w[3][:].indirect(l4[:]))
+        def product(name, tag, lhs_codes, lhs_scales, rhs_codes, rhs_scales):
+            bank = psum.tile([P, S], F32, name=name, tag=tag)
+            sums = bank[:, : rhs_codes.shape[1]]
+            nc.tensor.matmul_mx(out=sums, lhsT=lhs_codes.bitcast(FP8X4), lhsT_scale=lhs_scales,
+                                rhs=rhs_codes.bitcast(FP8X4), rhs_scale=rhs_scales, start=True, stop=True)
+            return sums
+
+        halves = [slice(0, W), slice(W, S)]
+        first = [product(f"y_ps0{h}", f"bank{4 * h}", w_c[:, :P], w_s[:, :P], xw_p[:, halves[h]], xs_p[:, halves[h]]) for h in range(2)]
+        for h in range(2):
+            nc.scalar.copy(y_w[0][:, halves[h]], first[h])
+        for h in range(2):
+            nc.scalar.mul(y_c[0][:, halves[h]], first[h], -1.0)
+        for t in range(1, PACK):
             cols = slice(t * P, (t + 1) * P)
-            nc.tensor.matmul_mx(out=y_ps[t][:], lhsT=w_c[:, cols].bitcast(FP8X4), lhsT_scale=w_s[:, cols],
-                                rhs=xw_p[:].bitcast(FP8X4), rhs_scale=xs_p[:], start=True, stop=True)
-            nc.scalar.copy(y_w[t][:, :S], y_ps[t][:])
-            nc.scalar.copy(y_c[t][:], y_ps[t][:])
+            sums = product(f"y_ps{t}", f"bank{t}", w_c[:, cols], w_s[:, cols], xw_p[:], xs_p[:])
+            nc.scalar.copy(y_w[t][:, :S], sums)
+            nc.scalar.mul(y_c[t][:], sums, -1.0)
 
         nst_w = planes("nst_w", WIDE)
-        y5 = planes("y5", S)
         nst2 = planes("nst2", S)
-        ytab = planes("ytab", S)
-        nsu = planes("nsu", S)
-        big = planes("big", S)
         zs = planes("zs", S)
         zh_w = planes("zh_w", WIDE)
         z2_f = sb.tile([P, PACK, S], F32, name="z2_f")
         z_f = sb.tile([P, PACK, S], F32, name="z_f")
-        for t in range(PACK):
-            nc.vector.tensor_tensor(nst_w[t][:, :S], y_w[t][:].indirect(l1[:]), y_c[t][:], ALU.subtract)
-            nc.vector.tensor_copy(y5[t][:], y_w[t][:].indirect(l5[:]))
-        for t in range(PACK):
-            nc.vector.tensor_tensor(ytab[t][:], tab_w[t][:].indirect(l4[:]), y_c[t][:], ALU.add)
-            nc.vector.tensor_copy(nst2[t][:], nst_w[t][:].indirect(l2[:]))
-        for t in range(PACK):
-            nc.vector.tensor_tensor(big[t][:], ytab[t][:], y5[t][:], ALU.max)
-            nc.scalar.activation(z2_f[:, t, :], big[t][:], ACT.Copy, scale=gb_sb[:, t : t + 1])
-        for t in range(PACK):
-            nc.vector.tensor_tensor(nsu[t][:], nst_w[t][:, :S], nst2[t][:], ALU.min)
-            nc.scalar.activation(zh_w[t][:, :S], nsu[t][:], ACT.Copy, scale=ga_neg_half[:, t : t + 1])
-            nc.scalar.activation(zs[t][:], nsu[t][:], ACT.Copy, scale=ga_neg[:, t : t + 1])
+        lead = planes("lead", S)
+        turned_sum = planes("turned_sum", S)
+        turned_relu = sb.tile([P, PACK, S], F32, name="turned_relu")
 
+        def turn_and_add(name, tag, first, second):
+            bank = psum.tile([P, S], F32, name=name, tag=tag)
+            for c in range(S // P):
+                cols = slice(c * P, (c + 1) * P)
+                nc.tensor.matmul(bank[:, cols], lhsT=first[:, cols], rhs=ident[:], is_transpose=True, start=True, stop=False)
+                nc.tensor.matmul(bank[:, cols], lhsT=second[:, cols], rhs=ident[:], is_transpose=True, start=False, stop=True)
+            return bank
+
+        def z2_plane(t):
+            bank = turn_and_add(f"back{t}", f"bank{6 + t % 2}", turned_sum[t], turned_relu[:, t, :])
+            nc.scalar.activation(z2_f[:, t, :], bank[:], ACT.Copy, scale=gb_sb[:, t : t + 1])
+
+        for t in range(PACK):
+            nc.vector.tensor_tensor(lead[t][:], y_w[t][:].indirect(l5[:]), tg[t][:], ALU.subtract)
+        for t in range(PACK):
+            nc.vector.tensor_tensor(nst_w[t][:, :S], y_w[t][:].indirect(l1[:]), y_c[t][:], ALU.add)
+        for t in range(PACK):
+            bank = turn_and_add(f"sum{t}", f"bank{t}", tg[t], y_w[t])
+            nc.scalar.copy(turned_sum[t][:], bank[:])
+            bank = turn_and_add(f"gap{t}", f"bank{4 + t % 2}", lead[t], y_c[t])
+            nc.scalar.activation(turned_relu[:, t, :], bank[:], ACT.Relu)
+            if t > 0:
+                z2_plane(t - 1)
+        z2_plane(PACK - 1)
         z2_bf = sb.tile([P, PACK * S], BF16, name="z2_bf", align_bytes=64)
-        nc.scalar.copy(z2_bf[:].rearrange("p (c i t) -> p c t i", i=4, t=PACK),
-                       z2_f[:].rearrange("p t (c i) -> p c t i", i=4))
+        z2_dst = z2_bf[:].rearrange("p (c i t) -> p c t i", i=4, t=PACK)
+        z2_src = z2_f[:].rearrange("p t (c i) -> p c t i", i=4)
+        for c in range(4):
+            nc.scalar.copy(z2_dst[:, 32 * c : 32 * (c + 1)], z2_src[:, 32 * c : 32 * (c + 1)])
+        nsu = [z2_f[:, 2 * (t % 2) : 2 * (t % 2) + 2, halves[t // 2]] for t in range(PACK)]
+
+        def in_two(ap):
+            return ap.rearrange("p (h c) -> p h c", h=2)
+
+        nc.scalar.mul(ga_neg[:], ga_sb[:], -1.0)
+        nc.scalar.mul(ga_neg_half[:], ga_sb[:], -0.5)
+
+        def larger(t):
+            nc.vector.tensor_tensor(nsu[t], in_two(nst_w[t][:, :S]), in_two(nst2[t][:]), ALU.min)
+            nc.scalar.activation(in_two(zh_w[t][:, :S]), nsu[t], ACT.Copy, scale=ga_neg_half[:, t : t + 1])
+            nc.scalar.activation(in_two(zs[t][:]), nsu[t], ACT.Copy, scale=ga_neg[:, t : t + 1])
+
+        for t in range(PACK):
+            nc.vector.tensor_copy(nst2[t][:], nst_w[t][:].indirect(l2[:]))
+            if t > 0:
+                larger(t - 1)
+        larger(PACK - 1)
+
         z2_c = sb.tile([P, S], U32, name="z2_c", align_bytes=64)
         z2_s = sb.tile([P, S], U8, name="z2_s", align_bytes=64)
 
         z_bf = sb.tile([P, PACK * S], BF16, name="z_bf", align_bytes=64)
         z_dst = z_bf[:].rearrange("p (u m t) -> p m t u", u=PACK, t=PACK)
         z_src = z_f[:].rearrange("p t (m u) -> p m t u", u=PACK)
+        nc.vector.quantize_mx(out=z2_c[:].bitcast(FP8X4), scales=z2_s[:], in_=z2_bf[:])
+        for t in range(PACK - 1):
+            nc.vector.tensor_tensor(z_f[:, t, :], zh_w[t][:].indirect(l3[:]), zs[t][:], ALU.add)
         for h in range(2):
-            cols = slice(h * 256, (h + 1) * 256)
-            for t in range(PACK):
-                nc.vector.tensor_tensor(z_f[:, t, cols], zh_w[t][:].indirect(l3[:, h * 16 : (h + 1) * 16]), zs[t][:, cols], ALU.add)
-            if h == 0:
-                nc.scalar.copy(z_dst[:, 0:64], z_src[:, 0:64])
-                nc.vector.quantize_mx(out=z2_c[:].bitcast(FP8X4), scales=z2_s[:], in_=z2_bf[:])
-            else:
-                nc.vector.tensor_copy(z_dst[:, 64:128], z_src[:, 64:128])
+            nc.vector.tensor_tensor(z_f[:, PACK - 1, halves[h]], zh_w[PACK - 1][:].indirect(l3[:, h * 16 : (h + 1) * 16]), zs[PACK - 1][:, halves[h]], ALU.add)
+        nc.scalar.copy(z_dst[:, 0:56], z_src[:, 0:56])
+        nc.vector.tensor_copy(z_dst[:, 56:128], z_src[:, 56:128])
 
         z_c = planes("z_c", P, U32)
         z_s = planes("z_s", P, U8)
-        s_ps = [psum.tile([P, S], F32, name=f"s_ps{u}") for u in range(PACK)]
         s_w = planes("s_w", S)
         pab = planes("pab", S)
         sq = planes("sq", S)
@@ -156,9 +202,13 @@ def tile_picked_selfthreekindpolar_none_p_kernel(
         out_rows = out.rearrange("(p u) c -> p u c", u=PACK)
         for u in range(PACK):
             nc.vector.quantize_mx(out=z_c[u][:].bitcast(FP8X4), scales=z_s[u][:], in_=z_bf[:, u * S : (u + 1) * S])
-            nc.tensor.matmul_mx(out=s_ps[u][:], lhsT=z_c[u][:].bitcast(FP8X4), lhsT_scale=z_s[u][:],
-                                rhs=z2_c[:].bitcast(FP8X4), rhs_scale=z2_s[:], start=True, stop=True)
-            nc.scalar.mul(s_w[u][:], s_ps[u][:], 0.0625)
+            if u == 0:
+                first = [product(f"s_ps0{h}", f"bank{4 * h}", z_c[0][:], z_s[0][:], z2_c[:, halves[h]], z2_s[:, halves[h]]) for h in range(2)]
+                nc.scalar.mul(s_w[0][:, halves[0]], first[0], 0.0625)
+                nc.vector.tensor_scalar(s_w[0][:, halves[1]], first[1], 0.0625, None, ALU.mult)
+            else:
+                sums = product(f"s_ps{u}", f"bank{u}", z_c[u][:], z_s[u][:], z2_c[:], z2_s[:])
+                nc.scalar.mul(s_w[u][:], sums, 0.0625)
 
         def fetch(u):
             nc.vector.tensor_copy(pab[u][:, :W], s_w[u][:].indirect(l6[:]))

@@ -76,7 +76,7 @@ def tile_picked_selfthreekindpolar_none_p_kernel(
 
         sq_w = planes("sq_w", S)
         for t in range(PACK):
-            nc.gpsimd.memset(sq_w[t][:], 0.0)
+            nc.vector.memset(sq_w[t][:], 0.0)
         tg = planes("tg", S)
         for t in range(3):
             nc.vector.tensor_copy(tg[t][:], tab_w[t][:].indirect(l4[:]))
@@ -90,9 +90,7 @@ def tile_picked_selfthreekindpolar_none_p_kernel(
         w_bf = sb.tile([P, PACK * H], BF16, name="w_bf", align_bytes=64)
         w_dst = w_bf[:].rearrange("p (t m j) -> p m j t", t=PACK, j=PACK)
         nc.scalar.copy(w_dst[:, 0:64], w_raw[0][:].rearrange("p j (m t) -> p m j t", t=PACK))
-        w_late = w_raw[1][:].rearrange("p j (m t) -> p m j t", t=PACK)
-        nc.scalar.copy(w_dst[:, 64:96], w_late[:, 0:32])
-        nc.vector.tensor_copy(w_dst[:, 96:128], w_late[:, 32:64])
+        nc.scalar.copy(w_dst[:, 64:128], w_raw[1][:].rearrange("p j (m t) -> p m j t", t=PACK))
         w_c = sb.tile([P, H], U32, name="w_c", align_bytes=64)
         w_s = sb.tile([P, H], U8, name="w_s", align_bytes=64)
         y_w = planes("y_w", WIDE)
@@ -112,13 +110,15 @@ def tile_picked_selfthreekindpolar_none_p_kernel(
         first = [product(f"y_ps0{h}", f"bank{4 * h}", w_c[:, :P], w_s[:, :P], xw_p[:, halves[h]], xs_p[:, halves[h]]) for h in range(2)]
         for h in range(2):
             nc.scalar.copy(y_w[0][:, halves[h]], first[h])
+        rest = []
+        for t in range(1, PACK):
+            cols = slice(t * P, (t + 1) * P)
+            rest.append(product(f"y_ps{t}", f"bank{t}", w_c[:, cols], w_s[:, cols], xw_p[:], xs_p[:]))
+            nc.scalar.copy(y_w[t][:, :S], rest[-1])
         for h in range(2):
             nc.scalar.mul(y_c[0][:, halves[h]], first[h], -1.0)
         for t in range(1, PACK):
-            cols = slice(t * P, (t + 1) * P)
-            sums = product(f"y_ps{t}", f"bank{t}", w_c[:, cols], w_s[:, cols], xw_p[:], xs_p[:])
-            nc.scalar.copy(y_w[t][:, :S], sums)
-            nc.scalar.mul(y_c[t][:], sums, -1.0)
+            nc.scalar.mul(y_c[t][:], rest[t - 1], -1.0)
 
         nst_w = planes("nst_w", WIDE)
         nst2 = planes("nst2", S)
@@ -139,7 +139,7 @@ def tile_picked_selfthreekindpolar_none_p_kernel(
             return bank
 
         def z2_plane(t):
-            bank = turn_and_add(f"back{t}", f"bank{6 + t % 2}", turned_sum[t], turned_relu[:, t, :])
+            bank = turn_and_add(f"back{t}", f"bank{4 + (t + 1) % 4}", turned_sum[t], turned_relu[:, t, :])
             nc.scalar.activation(z2_f[:, t, :], bank[:], ACT.Copy, scale=gb_sb[:, t : t + 1])
 
         for t in range(PACK):
@@ -147,22 +147,23 @@ def tile_picked_selfthreekindpolar_none_p_kernel(
         for t in range(PACK):
             nc.vector.tensor_tensor(nst_w[t][:, :S], y_w[t][:].indirect(l1[:]), y_c[t][:], ALU.add)
         for t in range(PACK):
-            bank = turn_and_add(f"sum{t}", f"bank{t}", tg[t], y_w[t])
+            bank = turn_and_add(f"sum{t}", f"bank{4 + (t + 1) % 4}", tg[t], y_w[t])
             nc.scalar.copy(turned_sum[t][:], bank[:])
-            bank = turn_and_add(f"gap{t}", f"bank{4 + t % 2}", lead[t], y_c[t])
+            bank = turn_and_add(f"gap{t}", f"bank{t}", lead[t], y_c[t])
             nc.scalar.activation(turned_relu[:, t, :], bank[:], ACT.Relu)
-            if t > 0:
-                z2_plane(t - 1)
+            if t >= 2:
+                z2_plane(t - 2)
+        z2_plane(PACK - 2)
         z2_plane(PACK - 1)
         z2_bf = sb.tile([P, PACK * S], BF16, name="z2_bf", align_bytes=64)
         z2_dst = z2_bf[:].rearrange("p (c i t) -> p c t i", i=4, t=PACK)
         z2_src = z2_f[:].rearrange("p t (c i) -> p c t i", i=4)
         for c in range(4):
             nc.scalar.copy(z2_dst[:, 32 * c : 32 * (c + 1)], z2_src[:, 32 * c : 32 * (c + 1)])
-        nsu = [z2_f[:, 2 * (t % 2) : 2 * (t % 2) + 2, halves[t // 2]] for t in range(PACK)]
+        nsu = [z2_f[:, :, t * P : (t + 1) * P] for t in range(PACK)]
 
         def in_two(ap):
-            return ap.rearrange("p (h c) -> p h c", h=2)
+            return ap.rearrange("p (h c) -> p h c", h=PACK)
 
         nc.scalar.mul(ga_neg[:], ga_sb[:], -1.0)
         nc.scalar.mul(ga_neg_half[:], ga_sb[:], -0.5)
@@ -189,8 +190,8 @@ def tile_picked_selfthreekindpolar_none_p_kernel(
             nc.vector.tensor_tensor(z_f[:, t, :], zh_w[t][:].indirect(l3[:]), zs[t][:], ALU.add)
         for h in range(2):
             nc.vector.tensor_tensor(z_f[:, PACK - 1, halves[h]], zh_w[PACK - 1][:].indirect(l3[:, h * 16 : (h + 1) * 16]), zs[PACK - 1][:, halves[h]], ALU.add)
-        nc.scalar.copy(z_dst[:, 0:56], z_src[:, 0:56])
-        nc.vector.tensor_copy(z_dst[:, 56:128], z_src[:, 56:128])
+        nc.scalar.copy(z_dst[:, 0:64], z_src[:, 0:64])
+        nc.vector.tensor_copy(z_dst[:, 64:128], z_src[:, 64:128])
 
         z_c = planes("z_c", P, U32)
         z_s = planes("z_s", P, U8)

@@ -49,20 +49,20 @@ def tile_picked_selfthreekindpolar_none_p_kernel(
         make_identity(nc, ident[:])
         tab_rows = tab.rearrange("(p t) c -> p t c", t=PACK)
         tab_w = planes("tab_w", WIDE)
+        w_rows = w1.rearrange("(p j) c -> p j c", j=PACK)
+        w_raw = [sb.tile([P, PACK, H // 2], F32, name=f"w_raw{h}") for h in range(2)]
+        xw = sb.tile([P, T], U32, name="xw", align_bytes=64)
         nc.sync.dma_start(tab_w[0][:, :S], tab_rows[:, 0, :])
         l4 = load_list(n4, "l4")
         l_offs = load_list(offs, "l_offs")
         l5 = load_list(n5, "l5")
         l1 = load_list(n1, "l1")
-        for t in range(1, 3):
-            nc.sync.dma_start(tab_w[t][:, :S], tab_rows[:, t, :])
-        w_rows = w1.rearrange("(p j) c -> p j c", j=PACK)
-        w_raw = [sb.tile([P, PACK, H // 2], F32, name=f"w_raw{h}") for h in range(2)]
+        nc.sync.dma_start(tab_w[1][:, :S], tab_rows[:, 1, :])
+        nc.sync.dma_start(tab_w[2][:, :S], tab_rows[:, 2, :])
         nc.sync.dma_start(w_raw[0][:], w_rows[:, :, :256])
         for q in range(4):
             nc.sync.dma_start(xs[32 * q : 32 * q + 4, :].bitcast(I32), x_scales[0, 4 * q : 4 * q + 4, :].bitcast(I32))
         nc.sync.dma_start(w_raw[1][:], w_rows[:, :, 256:])
-        xw = sb.tile([P, T], U32, name="xw", align_bytes=64)
         nc.sync.dma_start(xw[:].bitcast(I32), x_words[0].rearrange("p n t -> p (n t)").bitcast(I32))
         nc.sync.dma_start(tab_w[3][:, :S], tab_rows[:, 3, :])
         l2 = load_list(n2, "l2")
@@ -122,7 +122,8 @@ def tile_picked_selfthreekindpolar_none_p_kernel(
 
         nst_w = planes("nst_w", WIDE)
         nst2 = planes("nst2", S)
-        zs = planes("zs", S)
+        zs = [sb.tile([P, S], F32, name=f"zs{t}") for t in range(PACK - 1)]
+        zs_last = [sb.tile([P, W], F32, name=f"zs_last{h}", tag=f"zs_last{h}", align_bytes=64) for h in range(2)]
         zh_w = planes("zh_w", WIDE)
         z2_f = sb.tile([P, PACK, S], F32, name="z2_f")
         z_f = sb.tile([P, PACK, S], F32, name="z_f")
@@ -171,7 +172,11 @@ def tile_picked_selfthreekindpolar_none_p_kernel(
         def larger(t):
             nc.vector.tensor_tensor(nsu[t], in_two(nst_w[t][:, :S]), in_two(nst2[t][:]), ALU.min)
             nc.scalar.activation(in_two(zh_w[t][:, :S]), nsu[t], ACT.Copy, scale=ga_neg_half[:, t : t + 1])
-            nc.scalar.activation(in_two(zs[t][:]), nsu[t], ACT.Copy, scale=ga_neg[:, t : t + 1])
+            if t < PACK - 1:
+                nc.scalar.activation(in_two(zs[t][:]), nsu[t], ACT.Copy, scale=ga_neg[:, t : t + 1])
+            else:
+                for h in range(2):
+                    nc.scalar.activation(zs_last[h][:].rearrange("p (h c) -> p h c", h=2), nsu[t][:, 2 * h : 2 * h + 2], ACT.Copy, scale=ga_neg[:, t : t + 1])
 
         for t in range(PACK):
             nc.vector.tensor_copy(nst2[t][:], nst_w[t][:].indirect(l2[:]))
@@ -179,19 +184,21 @@ def tile_picked_selfthreekindpolar_none_p_kernel(
                 larger(t - 1)
         larger(PACK - 1)
 
-        z2_c = sb.tile([P, S], U32, name="z2_c", align_bytes=64)
         z2_s = sb.tile([P, S], U8, name="z2_s", align_bytes=64)
 
         z_bf = sb.tile([P, PACK * S], BF16, name="z_bf", align_bytes=64)
         z_dst = z_bf[:].rearrange("p (u m t) -> p m t u", u=PACK, t=PACK)
         z_src = z_f[:].rearrange("p t (m u) -> p m t u", u=PACK)
-        nc.vector.quantize_mx(out=z2_c[:].bitcast(FP8X4), scales=z2_s[:], in_=z2_bf[:])
         for t in range(PACK - 1):
             nc.vector.tensor_tensor(z_f[:, t, :], zh_w[t][:].indirect(l3[:]), zs[t][:], ALU.add)
         for h in range(2):
-            nc.vector.tensor_tensor(z_f[:, PACK - 1, halves[h]], zh_w[PACK - 1][:].indirect(l3[:, h * 16 : (h + 1) * 16]), zs[PACK - 1][:, halves[h]], ALU.add)
+            nc.vector.tensor_tensor(z_f[:, PACK - 1, halves[h]], zh_w[PACK - 1][:].indirect(l3[:, h * 16 : (h + 1) * 16]), zs_last[h][:], ALU.add)
+        z2_c = sb.tile([P, S], U32, name="z2_c", tag="zs_last0", align_bytes=64)
+        for h in range(2):
+            nc.vector.quantize_mx(out=z2_c[:, halves[h]].bitcast(FP8X4), scales=z2_s[:, halves[h]], in_=z2_bf[:, h * 1024 : (h + 1) * 1024])
+            if h == 0:
+                nc.vector.tensor_copy(z_dst[:, 64:128], z_src[:, 64:128])
         nc.scalar.copy(z_dst[:, 0:64], z_src[:, 0:64])
-        nc.vector.tensor_copy(z_dst[:, 64:128], z_src[:, 64:128])
 
         z_c = planes("z_c", P, U32)
         z_s = planes("z_s", P, U8)

@@ -18,7 +18,11 @@ ACT = mybir.ActivationFunctionType
 
 P = 128
 PACK = 4
-WIDE = 2 * S
+LAST = PACK - 1
+WINDOW = 2 * S
+HALVES = (slice(0, S // 2), slice(S // 2, S))
+LIST_HALVES = (slice(0, 16), slice(16, 32))
+S_SCALE = 0.0625
 
 
 def tile_picked_selfthreekindpolar_none_p_kernel(
@@ -31,40 +35,63 @@ def tile_picked_selfthreekindpolar_none_p_kernel(
         psum = ctx.enter_context(tc.psum_pool(name="psum", bufs=1))
 
         def load_list(src, name):
-            t = lists.tile(list(src.shape), U16, name=name)
-            nc.sync.dma_start(t[:], src)
-            return t
+            tile = lists.tile(list(src.shape), U16, name=name)
+            nc.sync.dma_start(tile[:], src)
+            return tile
 
-        def planes(name, width, dtype=F32):
+        def four_tiles(name, width, dtype=F32):
             return [sb.tile([P, width], dtype, name=f"{name}{t}", align_bytes=64) for t in range(PACK)]
 
-        quarter = sb.tile([P, 1], F32, name="quarter")
-        warm = sb.tile([P, 1], F32, name="warm")
-        nc.gpsimd.memset(quarter[:], 0.25)
-        nc.scalar.activation(warm[:], quarter[:], ACT.Sqrt)
+        def product(name, bank, lhs_codes, lhs_scales, rhs_codes, rhs_scales):
+            tile = psum.tile([P, S], F32, name=name, tag=f"bank{bank}")
+            sums = tile[:, : rhs_codes.shape[1]]
+            nc.tensor.matmul_mx(
+                out=sums,
+                lhsT=lhs_codes.bitcast(FP8X4),
+                lhsT_scale=lhs_scales,
+                rhs=rhs_codes.bitcast(FP8X4),
+                rhs_scale=rhs_scales,
+                start=True,
+                stop=True,
+            )
+            return sums
 
-        xs = sb.tile([P, T], U8, name="xs", align_bytes=64)
-        nc.gpsimd.memset(xs[:].bitcast(I32), 0)
+        def turn_and_add(name, bank, first, second):
+            tile = psum.tile([P, S], F32, name=name, tag=f"bank{bank}")
+            for c in range(S // P):
+                cols = slice(c * P, (c + 1) * P)
+                nc.tensor.matmul(tile[:, cols], lhsT=first[:, cols], rhs=ident[:], is_transpose=True, start=True, stop=False)
+                nc.tensor.matmul(tile[:, cols], lhsT=second[:, cols], rhs=ident[:], is_transpose=True, start=False, stop=True)
+            return tile
+
+        quarter = sb.tile([P, 1], F32, name="quarter")
+        nc.gpsimd.memset(quarter[:], 0.25)
+
+        x_scale_rows = sb.tile([P, T], U8, name="x_scale_rows", align_bytes=64)
+        nc.gpsimd.memset(x_scale_rows[:].bitcast(I32), 0)
         ident = sb.tile([P, P], F32, name="ident")
         make_identity(nc, ident[:])
+
         tab_rows = tab.rearrange("(p t) c -> p t c", t=PACK)
-        tab_w = planes("tab_w", WIDE)
+        tab_win = four_tiles("tab_win", WINDOW)
         w_rows = w1.rearrange("(p j) c -> p j c", j=PACK)
         w_raw = [sb.tile([P, PACK, H // 2], F32, name=f"w_raw{h}") for h in range(2)]
-        xw = sb.tile([P, T], U32, name="xw", align_bytes=64)
-        nc.sync.dma_start(tab_w[0][:, :S], tab_rows[:, 0, :])
+        x_word_rows = sb.tile([P, T], U32, name="x_word_rows", align_bytes=64)
+        nc.sync.dma_start(tab_win[0][:, :S], tab_rows[:, 0, :])
         l4 = load_list(n4, "l4")
         l_offs = load_list(offs, "l_offs")
         l5 = load_list(n5, "l5")
         l1 = load_list(n1, "l1")
-        nc.sync.dma_start(tab_w[1][:, :S], tab_rows[:, 1, :])
-        nc.sync.dma_start(tab_w[2][:, :S], tab_rows[:, 2, :])
-        nc.sync.dma_start(w_raw[0][:], w_rows[:, :, :256])
+        for t in range(1, LAST):
+            nc.sync.dma_start(tab_win[t][:, :S], tab_rows[:, t, :])
+        nc.sync.dma_start(w_raw[0][:], w_rows[:, :, HALVES[0]])
         for q in range(4):
-            nc.sync.dma_start(xs[32 * q : 32 * q + 4, :].bitcast(I32), x_scales[0, 4 * q : 4 * q + 4, :].bitcast(I32))
-        nc.sync.dma_start(w_raw[1][:], w_rows[:, :, 256:])
-        nc.sync.dma_start(xw[:].bitcast(I32), x_words[0].rearrange("p n t -> p (n t)").bitcast(I32))
-        nc.sync.dma_start(tab_w[3][:, :S], tab_rows[:, 3, :])
+            nc.sync.dma_start(
+                x_scale_rows[32 * q : 32 * q + 4, :].bitcast(I32), x_scales[0, 4 * q : 4 * q + 4, :].bitcast(I32)
+            )
+        nc.sync.dma_start(w_raw[1][:], w_rows[:, :, HALVES[1]])
+        nc.sync.dma_start(x_word_rows[:].bitcast(I32), x_words[0].rearrange("p n t -> p (n t)").bitcast(I32))
+        nc.sync.dma_start(tab_win[LAST][:, :S], tab_rows[:, LAST, :])
         l2 = load_list(n2, "l2")
         ga_sb = sb.tile([P, PACK], F32, name="ga_sb")
         gb_sb = sb.tile([P, PACK], F32, name="gb_sb")
@@ -74,168 +101,180 @@ def tile_picked_selfthreekindpolar_none_p_kernel(
         l6 = load_list(n6, "l6")
         l7 = load_list(n7, "l7")
 
-        sq_w = planes("sq_w", S)
-        for t in range(PACK):
-            nc.vector.memset(sq_w[t][:], 0.0)
-        tg = planes("tg", S)
-        for t in range(3):
-            nc.vector.tensor_copy(tg[t][:], tab_w[t][:].indirect(l4[:]))
-        ga_neg = sb.tile([P, PACK], F32, name="ga_neg")
-        ga_neg_half = sb.tile([P, PACK], F32, name="ga_neg_half")
+        squares_win = four_tiles("squares_win", S)
+        for u in range(PACK):
+            nc.vector.memset(squares_win[u][:], 0.0)
 
-        xw_p = sb.tile([P, S], U32, name="xw_p", align_bytes=64)
-        xs_p = sb.tile([P, S], U8, name="xs_p", align_bytes=64)
-        nc.vector.tensor_copy(xs_p[:], xs[:].indirect(l_offs[:]))
+        tab4 = four_tiles("tab4", S)
+        for t in range(LAST):
+            nc.vector.tensor_copy(tab4[t][:], tab_win[t][:].indirect(l4[:]))
 
-        w_bf = sb.tile([P, PACK * H], BF16, name="w_bf", align_bytes=64)
-        w_dst = w_bf[:].rearrange("p (t m j) -> p m j t", t=PACK, j=PACK)
-        nc.scalar.copy(w_dst[:, 0:64], w_raw[0][:].rearrange("p j (m t) -> p m j t", t=PACK))
-        nc.scalar.copy(w_dst[:, 64:128], w_raw[1][:].rearrange("p j (m t) -> p m j t", t=PACK))
-        w_c = sb.tile([P, H], U32, name="w_c", align_bytes=64)
-        w_s = sb.tile([P, H], U8, name="w_s", align_bytes=64)
-        y_w = planes("y_w", WIDE)
-        y_c = planes("y_c", S)
-        nc.vector.quantize_mx(out=w_c[:].bitcast(FP8X4), scales=w_s[:], in_=w_bf[:])
+        x_codes = sb.tile([P, S], U32, name="x_codes", align_bytes=64)
+        x_bytes = sb.tile([P, S], U8, name="x_bytes", align_bytes=64)
+        nc.vector.tensor_copy(x_bytes[:], x_scale_rows[:].indirect(l_offs[:]))
+        w_woven = sb.tile([P, PACK * H], BF16, name="w_woven", align_bytes=64)
+        w_dst = w_woven[:].rearrange("p (t m j) -> p m j t", t=PACK, j=PACK)
         for h in range(2):
-            nc.vector.tensor_copy(xw_p[:, h * W : (h + 1) * W], xw[:].indirect(l_offs[:, h * 16 : (h + 1) * 16]))
-        nc.vector.tensor_copy(tg[3][:], tab_w[3][:].indirect(l4[:]))
-        def product(name, tag, lhs_codes, lhs_scales, rhs_codes, rhs_scales):
-            bank = psum.tile([P, S], F32, name=name, tag=tag)
-            sums = bank[:, : rhs_codes.shape[1]]
-            nc.tensor.matmul_mx(out=sums, lhsT=lhs_codes.bitcast(FP8X4), lhsT_scale=lhs_scales,
-                                rhs=rhs_codes.bitcast(FP8X4), rhs_scale=rhs_scales, start=True, stop=True)
-            return sums
-
-        halves = [slice(0, W), slice(W, S)]
-        first = [product(f"y_ps0{h}", f"bank{4 * h}", w_c[:, :P], w_s[:, :P], xw_p[:, halves[h]], xs_p[:, halves[h]]) for h in range(2)]
+            nc.scalar.copy(w_dst[:, 64 * h : 64 * (h + 1)], w_raw[h][:].rearrange("p j (m t) -> p m j t", t=PACK))
+        w_codes = sb.tile([P, H], U32, name="w_codes", align_bytes=64)
+        w_bytes = sb.tile([P, H], U8, name="w_bytes", align_bytes=64)
+        nc.vector.quantize_mx(out=w_codes[:].bitcast(FP8X4), scales=w_bytes[:], in_=w_woven[:])
         for h in range(2):
-            nc.scalar.copy(y_w[0][:, halves[h]], first[h])
-        rest = []
+            nc.vector.tensor_copy(x_codes[:, HALVES[h]], x_word_rows[:].indirect(l_offs[:, LIST_HALVES[h]]))
+        nc.vector.tensor_copy(tab4[LAST][:], tab_win[LAST][:].indirect(l4[:]))
+
+        y_win = four_tiles("y_win", WINDOW)
+        y_neg = four_tiles("y_neg", S)
+        y_first = [
+            product(f"y0_{h}", PACK * h, w_codes[:, :P], w_bytes[:, :P], x_codes[:, HALVES[h]], x_bytes[:, HALVES[h]])
+            for h in range(2)
+        ]
+        for h in range(2):
+            nc.scalar.copy(y_win[0][:, HALVES[h]], y_first[h])
+        y_rest = {}
         for t in range(1, PACK):
             cols = slice(t * P, (t + 1) * P)
-            rest.append(product(f"y_ps{t}", f"bank{t}", w_c[:, cols], w_s[:, cols], xw_p[:], xs_p[:]))
-            nc.scalar.copy(y_w[t][:, :S], rest[-1])
+            y_rest[t] = product(f"y{t}", t, w_codes[:, cols], w_bytes[:, cols], x_codes[:], x_bytes[:])
+            nc.scalar.copy(y_win[t][:, :S], y_rest[t])
         for h in range(2):
-            nc.scalar.mul(y_c[0][:, halves[h]], first[h], -1.0)
+            nc.scalar.mul(y_neg[0][:, HALVES[h]], y_first[h], -1.0)
         for t in range(1, PACK):
-            nc.scalar.mul(y_c[t][:], rest[t - 1], -1.0)
+            nc.scalar.mul(y_neg[t][:], y_rest[t], -1.0)
 
-        nst_w = planes("nst_w", WIDE)
-        nst2 = planes("nst2", S)
-        zs = [sb.tile([P, S], F32, name=f"zs{t}") for t in range(PACK - 1)]
-        zs_last = [sb.tile([P, W], F32, name=f"zs_last{h}", tag=f"zs_last{h}", align_bytes=64) for h in range(2)]
-        zh_w = planes("zh_w", WIDE)
-        z2_f = sb.tile([P, PACK, S], F32, name="z2_f")
-        z_f = sb.tile([P, PACK, S], F32, name="z_f")
-        lead = planes("lead", S)
-        turned_sum = planes("turned_sum", S)
+        lead = four_tiles("lead", S)
+        st_neg_win = four_tiles("st_neg_win", WINDOW)
+        for t in range(PACK):
+            nc.vector.tensor_tensor(lead[t][:], y_win[t][:].indirect(l5[:]), tab4[t][:], ALU.subtract)
+        for t in range(PACK):
+            nc.vector.tensor_tensor(st_neg_win[t][:, :S], y_win[t][:].indirect(l1[:]), y_neg[t][:], ALU.add)
+
+        z2 = sb.tile([P, PACK, S], F32, name="z2")
+        turned_sum = four_tiles("turned_sum", S)
         turned_relu = sb.tile([P, PACK, S], F32, name="turned_relu")
 
-        def turn_and_add(name, tag, first, second):
-            bank = psum.tile([P, S], F32, name=name, tag=tag)
-            for c in range(S // P):
-                cols = slice(c * P, (c + 1) * P)
-                nc.tensor.matmul(bank[:, cols], lhsT=first[:, cols], rhs=ident[:], is_transpose=True, start=True, stop=False)
-                nc.tensor.matmul(bank[:, cols], lhsT=second[:, cols], rhs=ident[:], is_transpose=True, start=False, stop=True)
-            return bank
+        def sum_bank(t):
+            return PACK + (t + 1) % PACK
+
+        def z2_terms(t):
+            nc.scalar.copy(turned_sum[t][:], turn_and_add(f"sum{t}", sum_bank(t), tab4[t], y_win[t])[:])
+            nc.scalar.activation(turned_relu[:, t, :], turn_and_add(f"gap{t}", t, lead[t], y_neg[t])[:], ACT.Relu)
 
         def z2_plane(t):
-            bank = turn_and_add(f"back{t}", f"bank{4 + (t + 1) % 4}", turned_sum[t], turned_relu[:, t, :])
-            nc.scalar.activation(z2_f[:, t, :], bank[:], ACT.Copy, scale=gb_sb[:, t : t + 1])
+            larger = turn_and_add(f"back{t}", sum_bank(t), turned_sum[t], turned_relu[:, t, :])
+            nc.scalar.activation(z2[:, t, :], larger[:], ACT.Copy, scale=gb_sb[:, t : t + 1])
 
-        for t in range(PACK):
-            nc.vector.tensor_tensor(lead[t][:], y_w[t][:].indirect(l5[:]), tg[t][:], ALU.subtract)
-        for t in range(PACK):
-            nc.vector.tensor_tensor(nst_w[t][:, :S], y_w[t][:].indirect(l1[:]), y_c[t][:], ALU.add)
-        for t in range(PACK):
-            bank = turn_and_add(f"sum{t}", f"bank{4 + (t + 1) % 4}", tg[t], y_w[t])
-            nc.scalar.copy(turned_sum[t][:], bank[:])
-            bank = turn_and_add(f"gap{t}", f"bank{t}", lead[t], y_c[t])
-            nc.scalar.activation(turned_relu[:, t, :], bank[:], ACT.Relu)
-            if t >= 2:
-                z2_plane(t - 2)
-        z2_plane(PACK - 2)
-        z2_plane(PACK - 1)
-        z2_bf = sb.tile([P, PACK * S], BF16, name="z2_bf", align_bytes=64)
-        z2_dst = z2_bf[:].rearrange("p (c i t) -> p c t i", i=4, t=PACK)
-        z2_src = z2_f[:].rearrange("p t (c i) -> p c t i", i=4)
-        for c in range(4):
+        lag = 2
+        for step in range(PACK + lag):
+            if step < PACK:
+                z2_terms(step)
+            if step >= lag:
+                z2_plane(step - lag)
+
+        z2_woven = sb.tile([P, PACK * S], BF16, name="z2_woven", align_bytes=64)
+        z2_dst = z2_woven[:].rearrange("p (c i t) -> p c t i", i=4, t=PACK)
+        z2_src = z2[:].rearrange("p t (c i) -> p c t i", i=4)
+        for c in range(PACK):
             nc.scalar.copy(z2_dst[:, 32 * c : 32 * (c + 1)], z2_src[:, 32 * c : 32 * (c + 1)])
-        nsu = [z2_f[:, :, t * P : (t + 1) * P] for t in range(PACK)]
 
-        def in_two(ap):
-            return ap.rearrange("p (h c) -> p h c", h=PACK)
-
+        su_neg = [z2[:, :, t * P : (t + 1) * P] for t in range(PACK)]
+        st_neg2 = four_tiles("st_neg2", S)
+        ga_neg = sb.tile([P, PACK], F32, name="ga_neg")
+        ga_neg_half = sb.tile([P, PACK], F32, name="ga_neg_half")
         nc.scalar.mul(ga_neg[:], ga_sb[:], -1.0)
         nc.scalar.mul(ga_neg_half[:], ga_sb[:], -0.5)
+        half_win = four_tiles("half_win", WINDOW)
+        whole = [sb.tile([P, S], F32, name=f"whole{t}") for t in range(LAST)]
+        whole_last = [sb.tile([P, S // 2], F32, name=f"whole_last{h}", tag=f"whole_last{h}", align_bytes=64) for h in range(2)]
 
-        def larger(t):
-            nc.vector.tensor_tensor(nsu[t], in_two(nst_w[t][:, :S]), in_two(nst2[t][:]), ALU.min)
-            nc.scalar.activation(in_two(zh_w[t][:, :S]), nsu[t], ACT.Copy, scale=ga_neg_half[:, t : t + 1])
-            if t < PACK - 1:
-                nc.scalar.activation(in_two(zs[t][:]), nsu[t], ACT.Copy, scale=ga_neg[:, t : t + 1])
+        def in_runs(ap):
+            return ap.rearrange("p (r c) -> p r c", c=P)
+
+        def weigh_su(t):
+            nc.vector.tensor_tensor(su_neg[t], in_runs(st_neg_win[t][:, :S]), in_runs(st_neg2[t][:]), ALU.min)
+            nc.scalar.activation(in_runs(half_win[t][:, :S]), su_neg[t], ACT.Copy, scale=ga_neg_half[:, t : t + 1])
+            if t < LAST:
+                nc.scalar.activation(in_runs(whole[t][:]), su_neg[t], ACT.Copy, scale=ga_neg[:, t : t + 1])
             else:
                 for h in range(2):
-                    nc.scalar.activation(zs_last[h][:].rearrange("p (h c) -> p h c", h=2), nsu[t][:, 2 * h : 2 * h + 2], ACT.Copy, scale=ga_neg[:, t : t + 1])
+                    nc.scalar.activation(
+                        in_runs(whole_last[h][:]), su_neg[t][:, 2 * h : 2 * h + 2], ACT.Copy, scale=ga_neg[:, t : t + 1]
+                    )
 
-        for t in range(PACK):
-            nc.vector.tensor_copy(nst2[t][:], nst_w[t][:].indirect(l2[:]))
-            if t > 0:
-                larger(t - 1)
-        larger(PACK - 1)
+        for step in range(PACK + 1):
+            if step < PACK:
+                nc.vector.tensor_copy(st_neg2[step][:], st_neg_win[step][:].indirect(l2[:]))
+            if step >= 1:
+                weigh_su(step - 1)
 
-        z2_s = sb.tile([P, S], U8, name="z2_s", align_bytes=64)
-
-        z_bf = sb.tile([P, PACK * S], BF16, name="z_bf", align_bytes=64)
-        z_dst = z_bf[:].rearrange("p (u m t) -> p m t u", u=PACK, t=PACK)
-        z_src = z_f[:].rearrange("p t (m u) -> p m t u", u=PACK)
-        for t in range(PACK - 1):
-            nc.vector.tensor_tensor(z_f[:, t, :], zh_w[t][:].indirect(l3[:]), zs[t][:], ALU.add)
+        z = sb.tile([P, PACK, S], F32, name="z")
+        for t in range(LAST):
+            nc.vector.tensor_tensor(z[:, t, :], half_win[t][:].indirect(l3[:]), whole[t][:], ALU.add)
         for h in range(2):
-            nc.vector.tensor_tensor(z_f[:, PACK - 1, halves[h]], zh_w[PACK - 1][:].indirect(l3[:, h * 16 : (h + 1) * 16]), zs_last[h][:], ALU.add)
-        z2_c = sb.tile([P, S], U32, name="z2_c", tag="zs_last0", align_bytes=64)
-        for h in range(2):
-            nc.vector.quantize_mx(out=z2_c[:, halves[h]].bitcast(FP8X4), scales=z2_s[:, halves[h]], in_=z2_bf[:, h * 1024 : (h + 1) * 1024])
-            if h == 0:
-                nc.vector.tensor_copy(z_dst[:, 64:128], z_src[:, 64:128])
-        nc.scalar.copy(z_dst[:, 0:64], z_src[:, 0:64])
+            nc.vector.tensor_tensor(
+                z[:, LAST, HALVES[h]], half_win[LAST][:].indirect(l3[:, LIST_HALVES[h]]), whole_last[h][:], ALU.add
+            )
 
-        z_c = planes("z_c", P, U32)
-        z_s = planes("z_s", P, U8)
-        s_w = planes("s_w", S)
-        pab = planes("pab", S)
-        sq = planes("sq", S)
-        half = planes("half", W)
-        res = planes("res", S)
-        out_rows = out.rearrange("(p u) c -> p u c", u=PACK)
+        z2_codes = sb.tile([P, S], U32, name="z2_codes", tag="whole_last0", align_bytes=64)
+        z2_bytes = sb.tile([P, S], U8, name="z2_bytes", align_bytes=64)
+        z_woven = sb.tile([P, PACK * S], BF16, name="z_woven", align_bytes=64)
+        z_dst = z_woven[:].rearrange("p (u m t) -> p m t u", u=PACK, t=PACK)
+        z_src = z[:].rearrange("p t (m u) -> p m t u", u=PACK)
+
+        def quantise_z2(h):
+            nc.vector.quantize_mx(
+                out=z2_codes[:, HALVES[h]].bitcast(FP8X4),
+                scales=z2_bytes[:, HALVES[h]],
+                in_=z2_woven[:, h * 2 * S : (h + 1) * 2 * S],
+            )
+
+        quantise_z2(0)
+        nc.vector.tensor_copy(z_dst[:, 64:128, :, 0:2], z_src[:, 64:128, :, 0:2])
+        quantise_z2(1)
+        nc.scalar.copy(z_dst[:, 0:64, :, 0:2], z_src[:, 0:64, :, 0:2])
+        nc.scalar.copy(z_dst[:, :, :, 2:4], z_src[:, :, :, 2:4])
+
+        z_codes = four_tiles("z_codes", P, U32)
+        z_bytes = four_tiles("z_bytes", P, U8)
+        s_win = four_tiles("s_win", S)
         for u in range(PACK):
-            nc.vector.quantize_mx(out=z_c[u][:].bitcast(FP8X4), scales=z_s[u][:], in_=z_bf[:, u * S : (u + 1) * S])
+            nc.vector.quantize_mx(
+                out=z_codes[u][:].bitcast(FP8X4), scales=z_bytes[u][:], in_=z_woven[:, u * S : (u + 1) * S]
+            )
             if u == 0:
-                first = [product(f"s_ps0{h}", f"bank{4 * h}", z_c[0][:], z_s[0][:], z2_c[:, halves[h]], z2_s[:, halves[h]]) for h in range(2)]
-                nc.scalar.mul(s_w[0][:, halves[0]], first[0], 0.0625)
-                nc.vector.tensor_scalar(s_w[0][:, halves[1]], first[1], 0.0625, None, ALU.mult)
+                s_first = [
+                    product(f"s0_{h}", PACK * h, z_codes[0][:], z_bytes[0][:], z2_codes[:, HALVES[h]], z2_bytes[:, HALVES[h]])
+                    for h in range(2)
+                ]
+                nc.scalar.mul(s_win[0][:, HALVES[0]], s_first[0], S_SCALE)
+                nc.vector.tensor_scalar(s_win[0][:, HALVES[1]], s_first[1], S_SCALE, None, ALU.mult)
             else:
-                sums = product(f"s_ps{u}", f"bank{u}", z_c[u][:], z_s[u][:], z2_c[:], z2_s[:])
-                nc.scalar.mul(s_w[u][:], sums, 0.0625)
+                sums = product(f"s{u}", u, z_codes[u][:], z_bytes[u][:], z2_codes[:], z2_bytes[:])
+                nc.scalar.mul(s_win[u][:], sums, S_SCALE)
 
-        def fetch(u):
-            nc.vector.tensor_copy(pab[u][:, :W], s_w[u][:].indirect(l6[:]))
-            nc.vector.tensor_copy(pab[u][:, W:], s_w[u][:].indirect(l7[:]))
-            nc.scalar.activation(sq[u][:], pab[u][:], ACT.Square)
-            nc.scalar.mul(half[u][:], pab[u][:, :W], -0.5)
+        pa_pb = four_tiles("pa_pb", 2 * W)
+        squares = four_tiles("squares", 2 * W)
+        pa_neg_half = four_tiles("pa_neg_half", W)
+        result = four_tiles("result", S)
+        out_rows = out.rearrange("(p u) c -> p u c", u=PACK)
 
-        def put_radius(u):
-            nc.vector.tensor_tensor(sq_w[u][:].indirect(l6[:]), sq[u][:, :W], sq[u][:, W:], ALU.add)
-            nc.scalar.activation(res[u][:], sq_w[u][:], ACT.Sqrt, bias=quarter[:])
+        def fetch_pairs(u):
+            nc.vector.tensor_copy(pa_pb[u][:, :W], s_win[u][:].indirect(l6[:]))
+            nc.vector.tensor_copy(pa_pb[u][:, W:], s_win[u][:].indirect(l7[:]))
+            nc.scalar.activation(squares[u][:], pa_pb[u][:], ACT.Square)
+            nc.scalar.mul(pa_neg_half[u][:], pa_pb[u][:, :W], -0.5)
 
-        def put_rest(u):
-            nc.vector.tensor_tensor(res[u][:].indirect(l7[:]), pab[u][:, W:], half[u][:], ALU.add)
-            nc.sync.dma_start(out_rows[:, u, :], res[u][:])
+        def put_ra(u):
+            nc.vector.tensor_tensor(squares_win[u][:].indirect(l6[:]), squares[u][:, :W], squares[u][:, W:], ALU.add)
+            nc.scalar.activation(result[u][:], squares_win[u][:], ACT.Sqrt, bias=quarter[:])
+
+        def put_rb(u):
+            nc.vector.tensor_tensor(result[u][:].indirect(l7[:]), pa_pb[u][:, W:], pa_neg_half[u][:], ALU.add)
+            nc.sync.dma_start(out_rows[:, u, :], result[u][:])
 
         for step in range(PACK + 2):
             if step < PACK:
-                fetch(step)
+                fetch_pairs(step)
             if 1 <= step <= PACK:
-                put_radius(step - 1)
+                put_ra(step - 1)
             if step >= 2:
-                put_rest(step - 2)
+                put_rb(step - 2)

from contextlib import ExitStack

import concourse.mybir as mybir
from concourse.masks import make_identity

K, T, S, H, W = 512, 2048, 512, 512, 256
FLOPS = 2 * K * H * S + 2 * H * S * S

F32 = mybir.dt.float32
BF16 = mybir.dt.bfloat16
I32 = mybir.dt.int32
U32 = mybir.dt.uint32
U16 = mybir.dt.uint16
U8 = mybir.dt.uint8
FP8X4 = mybir.dt.float8_e4m3fn_x4
ALU = mybir.AluOpType
ACT = mybir.ActivationFunctionType

P = 128
PACK = 4
LAST = PACK - 1
WINDOW = 2 * S
HALVES = (slice(0, S // 2), slice(S // 2, S))
LIST_HALVES = (slice(0, 16), slice(16, 32))
S_SCALE = 0.0625


def tile_picked_selfthreekindpolar_none_p_kernel(
    tc, x_words, x_scales, w1, tab, ga, gb, offs, n1, n2, n3, n4, n5, n6, n7, out
):
    nc = tc.nc
    with ExitStack() as ctx:
        lists = ctx.enter_context(tc.tile_pool(name="lists", bufs=1))
        sb = ctx.enter_context(tc.tile_pool(name="sb", bufs=1))
        psum = ctx.enter_context(tc.psum_pool(name="psum", bufs=1))

        def load_list(src, name):
            tile = lists.tile(list(src.shape), U16, name=name)
            nc.sync.dma_start(tile[:], src)
            return tile

        def four_tiles(name, width, dtype=F32):
            return [sb.tile([P, width], dtype, name=f"{name}{t}", align_bytes=64) for t in range(PACK)]

        def product(name, bank, lhs_codes, lhs_scales, rhs_codes, rhs_scales):
            tile = psum.tile([P, S], F32, name=name, tag=f"bank{bank}")
            sums = tile[:, : rhs_codes.shape[1]]
            nc.tensor.matmul_mx(
                out=sums,
                lhsT=lhs_codes.bitcast(FP8X4),
                lhsT_scale=lhs_scales,
                rhs=rhs_codes.bitcast(FP8X4),
                rhs_scale=rhs_scales,
                start=True,
                stop=True,
            )
            return sums

        def turn_and_add(name, bank, first, second):
            tile = psum.tile([P, S], F32, name=name, tag=f"bank{bank}")
            for c in range(S // P):
                cols = slice(c * P, (c + 1) * P)
                nc.tensor.matmul(tile[:, cols], lhsT=first[:, cols], rhs=ident[:], is_transpose=True, start=True, stop=False)
                nc.tensor.matmul(tile[:, cols], lhsT=second[:, cols], rhs=ident[:], is_transpose=True, start=False, stop=True)
            return tile

        quarter = sb.tile([P, 1], F32, name="quarter")
        nc.gpsimd.memset(quarter[:], 0.25)

        x_scale_rows = sb.tile([P, T], U8, name="x_scale_rows", align_bytes=64)
        nc.gpsimd.memset(x_scale_rows[:].bitcast(I32), 0)
        ident = sb.tile([P, P], F32, name="ident")
        make_identity(nc, ident[:])

        tab_rows = tab.rearrange("(p t) c -> p t c", t=PACK)
        tab_win = four_tiles("tab_win", WINDOW)
        w_rows = w1.rearrange("(p j) c -> p j c", j=PACK)
        w_raw = [sb.tile([P, PACK, H // 2], F32, name=f"w_raw{h}") for h in range(2)]
        x_word_rows = sb.tile([P, T], U32, name="x_word_rows", align_bytes=64)
        nc.sync.dma_start(tab_win[0][:, :S], tab_rows[:, 0, :])
        l4 = load_list(n4, "l4")
        l_offs = load_list(offs, "l_offs")
        l5 = load_list(n5, "l5")
        l1 = load_list(n1, "l1")
        for t in range(1, LAST):
            nc.sync.dma_start(tab_win[t][:, :S], tab_rows[:, t, :])
        nc.sync.dma_start(w_raw[0][:], w_rows[:, :, HALVES[0]])
        for q in range(4):
            nc.sync.dma_start(
                x_scale_rows[32 * q : 32 * q + 4, :].bitcast(I32), x_scales[0, 4 * q : 4 * q + 4, :].bitcast(I32)
            )
        nc.sync.dma_start(w_raw[1][:], w_rows[:, :, HALVES[1]])
        nc.sync.dma_start(x_word_rows[:].bitcast(I32), x_words[0].rearrange("p n t -> p (n t)").bitcast(I32))
        nc.sync.dma_start(tab_win[LAST][:, :S], tab_rows[:, LAST, :])
        l2 = load_list(n2, "l2")
        ga_sb = sb.tile([P, PACK], F32, name="ga_sb")
        gb_sb = sb.tile([P, PACK], F32, name="gb_sb")
        nc.sync.dma_start(gb_sb[:], gb.rearrange("(p t) o -> p (t o)", t=PACK))
        nc.sync.dma_start(ga_sb[:], ga.rearrange("(p t) o -> p (t o)", t=PACK))
        l3 = load_list(n3, "l3")
        l6 = load_list(n6, "l6")
        l7 = load_list(n7, "l7")

        squares_win = four_tiles("squares_win", S)
        for u in range(PACK):
            nc.vector.memset(squares_win[u][:], 0.0)

        tab4 = four_tiles("tab4", S)
        for t in range(LAST):
            nc.vector.tensor_copy(tab4[t][:], tab_win[t][:].indirect(l4[:]))

        x_codes = sb.tile([P, S], U32, name="x_codes", align_bytes=64)
        x_bytes = sb.tile([P, S], U8, name="x_bytes", align_bytes=64)
        nc.vector.tensor_copy(x_bytes[:], x_scale_rows[:].indirect(l_offs[:]))
        w_woven = sb.tile([P, PACK * H], BF16, name="w_woven", align_bytes=64)
        w_dst = w_woven[:].rearrange("p (t m j) -> p m j t", t=PACK, j=PACK)
        for h in range(2):
            nc.scalar.copy(w_dst[:, 64 * h : 64 * (h + 1)], w_raw[h][:].rearrange("p j (m t) -> p m j t", t=PACK))
        w_codes = sb.tile([P, H], U32, name="w_codes", align_bytes=64)
        w_bytes = sb.tile([P, H], U8, name="w_bytes", align_bytes=64)
        nc.vector.quantize_mx(out=w_codes[:].bitcast(FP8X4), scales=w_bytes[:], in_=w_woven[:])
        for h in range(2):
            nc.vector.tensor_copy(x_codes[:, HALVES[h]], x_word_rows[:].indirect(l_offs[:, LIST_HALVES[h]]))
        nc.vector.tensor_copy(tab4[LAST][:], tab_win[LAST][:].indirect(l4[:]))

        y_win = four_tiles("y_win", WINDOW)
        y_neg = four_tiles("y_neg", S)
        y_first = [
            product(f"y0_{h}", PACK * h, w_codes[:, :P], w_bytes[:, :P], x_codes[:, HALVES[h]], x_bytes[:, HALVES[h]])
            for h in range(2)
        ]
        for h in range(2):
            nc.scalar.copy(y_win[0][:, HALVES[h]], y_first[h])
        y_rest = {}
        for t in range(1, PACK):
            cols = slice(t * P, (t + 1) * P)
            y_rest[t] = product(f"y{t}", t, w_codes[:, cols], w_bytes[:, cols], x_codes[:], x_bytes[:])
            nc.scalar.copy(y_win[t][:, :S], y_rest[t])
        for h in range(2):
            nc.scalar.mul(y_neg[0][:, HALVES[h]], y_first[h], -1.0)
        for t in range(1, PACK):
            nc.scalar.mul(y_neg[t][:], y_rest[t], -1.0)

        lead = four_tiles("lead", S)
        st_neg_win = four_tiles("st_neg_win", WINDOW)
        for t in range(PACK):
            nc.vector.tensor_tensor(lead[t][:], y_win[t][:].indirect(l5[:]), tab4[t][:], ALU.subtract)
        for t in range(PACK):
            nc.vector.tensor_tensor(st_neg_win[t][:, :S], y_win[t][:].indirect(l1[:]), y_neg[t][:], ALU.add)

        z2 = sb.tile([P, PACK, S], F32, name="z2")
        turned_sum = four_tiles("turned_sum", S)
        turned_relu = sb.tile([P, PACK, S], F32, name="turned_relu")

        def sum_bank(t):
            return PACK + (t + 1) % PACK

        def z2_terms(t):
            nc.scalar.copy(turned_sum[t][:], turn_and_add(f"sum{t}", sum_bank(t), tab4[t], y_win[t])[:])
            nc.scalar.activation(turned_relu[:, t, :], turn_and_add(f"gap{t}", t, lead[t], y_neg[t])[:], ACT.Relu)

        def z2_plane(t):
            larger = turn_and_add(f"back{t}", sum_bank(t), turned_sum[t], turned_relu[:, t, :])
            nc.scalar.activation(z2[:, t, :], larger[:], ACT.Copy, scale=gb_sb[:, t : t + 1])

        lag = 2
        for step in range(PACK + lag):
            if step < PACK:
                z2_terms(step)
            if step >= lag:
                z2_plane(step - lag)

        z2_woven = sb.tile([P, PACK * S], BF16, name="z2_woven", align_bytes=64)
        z2_dst = z2_woven[:].rearrange("p (c i t) -> p c t i", i=4, t=PACK)
        z2_src = z2[:].rearrange("p t (c i) -> p c t i", i=4)
        for c in range(PACK):
            nc.scalar.copy(z2_dst[:, 32 * c : 32 * (c + 1)], z2_src[:, 32 * c : 32 * (c + 1)])

        su_neg = [z2[:, :, t * P : (t + 1) * P] for t in range(PACK)]
        st_neg2 = four_tiles("st_neg2", S)
        ga_neg = sb.tile([P, PACK], F32, name="ga_neg")
        ga_neg_half = sb.tile([P, PACK], F32, name="ga_neg_half")
        nc.scalar.mul(ga_neg[:], ga_sb[:], -1.0)
        nc.scalar.mul(ga_neg_half[:], ga_sb[:], -0.5)
        half_win = four_tiles("half_win", WINDOW)
        whole = [sb.tile([P, S], F32, name=f"whole{t}") for t in range(LAST)]
        whole_last = [sb.tile([P, S // 2], F32, name=f"whole_last{h}", tag=f"whole_last{h}", align_bytes=64) for h in range(2)]

        def in_runs(ap):
            return ap.rearrange("p (r c) -> p r c", c=P)

        def weigh_su(t):
            nc.vector.tensor_tensor(su_neg[t], in_runs(st_neg_win[t][:, :S]), in_runs(st_neg2[t][:]), ALU.min)
            nc.scalar.activation(in_runs(half_win[t][:, :S]), su_neg[t], ACT.Copy, scale=ga_neg_half[:, t : t + 1])
            if t < LAST:
                nc.scalar.activation(in_runs(whole[t][:]), su_neg[t], ACT.Copy, scale=ga_neg[:, t : t + 1])
            else:
                for h in range(2):
                    nc.scalar.activation(
                        in_runs(whole_last[h][:]), su_neg[t][:, 2 * h : 2 * h + 2], ACT.Copy, scale=ga_neg[:, t : t + 1]
                    )

        for step in range(PACK + 1):
            if step < PACK:
                nc.vector.tensor_copy(st_neg2[step][:], st_neg_win[step][:].indirect(l2[:]))
            if step >= 1:
                weigh_su(step - 1)

        z = sb.tile([P, PACK, S], F32, name="z")
        for t in range(LAST):
            nc.vector.tensor_tensor(z[:, t, :], half_win[t][:].indirect(l3[:]), whole[t][:], ALU.add)
        for h in range(2):
            nc.vector.tensor_tensor(
                z[:, LAST, HALVES[h]], half_win[LAST][:].indirect(l3[:, LIST_HALVES[h]]), whole_last[h][:], ALU.add
            )

        z2_codes = sb.tile([P, S], U32, name="z2_codes", tag="whole_last0", align_bytes=64)
        z2_bytes = sb.tile([P, S], U8, name="z2_bytes", align_bytes=64)
        z_woven = sb.tile([P, PACK * S], BF16, name="z_woven", align_bytes=64)
        z_dst = z_woven[:].rearrange("p (u m t) -> p m t u", u=PACK, t=PACK)
        z_src = z[:].rearrange("p t (m u) -> p m t u", u=PACK)

        def quantise_z2(h):
            nc.vector.quantize_mx(
                out=z2_codes[:, HALVES[h]].bitcast(FP8X4),
                scales=z2_bytes[:, HALVES[h]],
                in_=z2_woven[:, h * 2 * S : (h + 1) * 2 * S],
            )

        quantise_z2(0)
        nc.vector.tensor_copy(z_dst[:, 64:128, :, 0:2], z_src[:, 64:128, :, 0:2])
        quantise_z2(1)
        nc.scalar.copy(z_dst[:, 0:64, :, 0:2], z_src[:, 0:64, :, 0:2])
        nc.scalar.copy(z_dst[:, :, :, 2:4], z_src[:, :, :, 2:4])

        z_codes = four_tiles("z_codes", P, U32)
        z_bytes = four_tiles("z_bytes", P, U8)
        s_win = four_tiles("s_win", S)
        for u in range(PACK):
            nc.vector.quantize_mx(
                out=z_codes[u][:].bitcast(FP8X4), scales=z_bytes[u][:], in_=z_woven[:, u * S : (u + 1) * S]
            )
            if u == 0:
                s_first = [
                    product(f"s0_{h}", PACK * h, z_codes[0][:], z_bytes[0][:], z2_codes[:, HALVES[h]], z2_bytes[:, HALVES[h]])
                    for h in range(2)
                ]
                nc.scalar.mul(s_win[0][:, HALVES[0]], s_first[0], S_SCALE)
                nc.vector.tensor_scalar(s_win[0][:, HALVES[1]], s_first[1], S_SCALE, None, ALU.mult)
            else:
                sums = product(f"s{u}", u, z_codes[u][:], z_bytes[u][:], z2_codes[:], z2_bytes[:])
                nc.scalar.mul(s_win[u][:], sums, S_SCALE)

        pa_pb = four_tiles("pa_pb", 2 * W)
        squares = four_tiles("squares", 2 * W)
        pa_neg_half = four_tiles("pa_neg_half", W)
        result = four_tiles("result", S)
        out_rows = out.rearrange("(p u) c -> p u c", u=PACK)

        def fetch_pairs(u):
            nc.vector.tensor_copy(pa_pb[u][:, :W], s_win[u][:].indirect(l6[:]))
            nc.vector.tensor_copy(pa_pb[u][:, W:], s_win[u][:].indirect(l7[:]))
            nc.scalar.activation(squares[u][:], pa_pb[u][:], ACT.Square)
            nc.scalar.mul(pa_neg_half[u][:], pa_pb[u][:, :W], -0.5)

        def put_ra(u):
            nc.vector.tensor_tensor(squares_win[u][:].indirect(l6[:]), squares[u][:, :W], squares[u][:, W:], ALU.add)
            nc.scalar.activation(result[u][:], squares_win[u][:], ACT.Sqrt, bias=quarter[:])

        def put_rb(u):
            nc.vector.tensor_tensor(result[u][:].indirect(l7[:]), pa_pb[u][:, W:], pa_neg_half[u][:], ALU.add)
            nc.sync.dma_start(out_rows[:, u, :], result[u][:])

        for step in range(PACK + 2):
            if step < PACK:
                fetch_pairs(step)
            if 1 <= step <= PACK:
                put_ra(step - 1)
            if step >= 2:
                put_rb(step - 2)
